import numpy as np, ml_dtypes
CORES = [17,81,89,18,82,90]
N = 6
import mx_ref
NC = 128
BF = ml_dtypes.bfloat16
def cut(t, i, w=512):
    return t[:, w * i:w * i + w]
def term(a, B):
    return np.stack([np.maximum(mx_ref.matmul(mx_ref.quantize(cut(a, i)), B), 0) for i in range(4)], axis=2).reshape(128, -1)
def setup_inputs(rng):
    def f(*shape):
        return mx_ref.flush((rng.standard_normal(shape, dtype=np.float32) * np.exp2(rng.integers(-2, 3, shape[:-1] + (1,)))).astype(BF))
    return {"a": f(N, 128, 4 * 512), "b": f(N, 128, 4 * NC)}
def setup_inputs_blocks(rng):
    d = setup_inputs(rng)
    for k in ("a", "b"): d[k] = mx_ref.spread(d[k], rng, 2)
    return d
def setup_inputs_wide(rng):
    d = setup_inputs(rng)
    for k in ("a", "b"): d[k] = mx_ref.flush((d[k].astype(np.float32) * np.exp2(rng.integers(-4, 5, (N, 1, 1))).astype(np.float32)).astype(BF))
    return d
def setup_inputs_lossless(rng):
    a = np.zeros((N, 128, 4 * 128, 4), np.float32)
    for r in range(N):
        k = rng.integers(0, 512, size=4 * 128)
        a[r, k // 4, np.arange(4 * 128), k % 4] = 1.0
    size = np.repeat(2.0 ** rng.integers(-4, 5, size=(1, 1, (4 * NC) // 4)), 4, axis=2)
    b = (rng.random((N, 128, 4 * NC)) < 0.8) * size
    return {"a": a.reshape(N, 128, 4 * 512).astype(BF), "b": b.astype(np.float32).astype(BF)}
def reference(a, b):
    Bq = [mx_ref.quantize(b[c]) for c in range(N)]
    y = np.zeros((N, 128, 4 * NC), np.float32)
    for c in range(N):
        y[c] = mx_ref.total([term(a[r], Bq[c]) for r in range(N)])
    return {"y": y}

from concourse.bass import DstId, RemoteDMATransfer
from concourse.mybir import dt, AluOpType, ActivationFunctionType

SIM_CORES = 96
W = 128
RING = 4

SCRATCH = {
    "ta": ("sbuf", [128, 2048], "bfloat16"),
    "tb": ("sbuf", [128, 512], "bfloat16"),
    "qa": ("sbuf", [128, 512], "float8_e4m3fn_x4"),
    "sa": ("sbuf", [128, 512], "uint8"),
    "qb": ("sbuf", [128, 128], "float8_e4m3fn_x4"),
    "sb": ("sbuf", [128, 128], "uint8"),
    "qrl": ("sbuf", [128, 128], "float8_e4m3fn_x4"),
    "srl": ("sbuf", [128, 128], "uint8"),
    "qfa": ("sbuf", [128, 1024], "float8_e4m3fn_x4"),
    "sfa": ("sbuf", [128, 1024], "uint8"),
    "qfb": ("sbuf", [128, 256], "float8_e4m3fn_x4"),
    "sfb": ("sbuf", [128, 256], "uint8"),
    "t": ("sbuf", [128, 4096], "bfloat16"),
    "tile": ("sbuf", [128, 2048], "bfloat16"),
    "qp": ("sbuf", [128, 512], "float8_e4m3fn_x4"),
    "sp": ("sbuf", [128, 512], "uint8"),
    "qfp": ("sbuf", [128, 384], "float8_e4m3fn_x4"),
    "sfp": ("sbuf", [128, 384], "uint8"),
    "dsel": ("sbuf", [128, 516], "bfloat16"),
    "qsel": ("sbuf", [128, 512], "float8_e4m3fn_x4"),
    "ssel": ("sbuf", [128, 512], "uint8"),
    "yt": ("sbuf", [128, 512], "float32"),
    "pr": ("psum", [128, 512 * RING], "float32"),
    "fin": ("psum", [128, 2048], "float32"),
}
SEMAPHORES = ["lb", "la0", "la1", "ms", "ds", "vq", "va", "pe", "sc", "fin", "yd", "st", "sent", "rl",
              "fb0", "fb1", "fa00", "fa01", "fa10", "fa11", "fp0", "fp1", "fp2"]


def _engines(mask):
    return [e for e in range(16) if mask >> e & 1]


def _share(mask, n):
    e = _engines(mask)
    k = 1
    while 2 * k * n <= len(e):
        k *= 2
    return [sum(1 << x for x in e[i * k:i * k + k]) for i in range(n)]


def _plan(T, topo):
    ranks = list(T.cores)
    chips = []
    for r in ranks:
        if topo.chip(r) not in chips:
            chips.append(topo.chip(r))
    here = {x: [r for r in ranks if topo.chip(r) == x] for x in chips}

    def reach(k, y):
        return all(topo.may_write(k, d) for d in here[y])

    ex, relay = {}, {}
    for x in chips:
        far = [y for y in chips if y != x]
        relay[x] = [k for k in here[x] if all(reach(k, y) for y in far)][0]
        used = []
        for y in sorted(far, key=lambda z: len([k for k in here[x] if reach(k, z)])):
            can = [k for k in here[x] if reach(k, y) and k not in used]
            if not can:
                can = [k for k in range(SIM_CORES) if topo.chip(k) == x and k not in ranks and k not in used
                       and reach(k, y) and topo.die(k) == topo.die(relay[x])]
            ex[x, y] = can[0]
            used.append(can[0])
    execs = {x: [ex[x, y] for y in chips if y != x] for x in chips}
    seq = {x: sorted(here[x], key=lambda k: k != relay[x]) for x in chips}
    foreign = {e: [r for r in here[x] if r != e] for x in chips for e in set(execs[x] + here[x])}
    pieces = {r: ([(0, 4)] if r == relay[topo.chip(r)] else [(0, 2), (2, 4)]) for r in ranks}

    jobs = {}
    for x in chips:
        for e in foreign:
            if topo.chip(e) != x:
                continue
            own = [e] if e in here[x] else []
            js = []
            if e in own:
                for r in here[x]:
                    if r != e and r not in execs[x]:
                        js.append(("rl", 0, own, r))
            for y in chips:
                if y != x and ex[x, y] == e:
                    js += [("fb", k, own + foreign[e], c) for k, c in enumerate(seq[y])]
            if own:
                js.append(("b", 0, own + (foreign[e] if e in execs[x] else []), e))
            jobs[e] = js

    sources = {}
    for c in ranks:
        x = topo.chip(c)
        src = [e for e in foreign if e != c and any(j[3] == c for j in jobs[e])]
        sources[c] = sorted(src, key=lambda e: 0 if topo.chip(e) == x else 1 if topo.may_write(c, e) else 2)

    sends = {}
    for e in foreign:
        x = topo.chip(e)
        peer = [k for k in foreign if topo.chip(k) == x and k != e][0]
        away = here[[y for y in chips if y != x][0]][0]
        chipm, offm = topo.mask(e, peer), topo.mask(e, away)
        upper = chipm & ~offm
        gs = []
        if e in ranks:
            far = [ex[y, x] for y in chips if y != x]
            slot = seq[x].index(e)
            if e != relay[x]:
                m = _share(upper, 1)[0]
                gs.append((("q", "b"), [(relay[x], "b", 0, "rl", 0, W, "rl", m)]))
            direct = [d for d in far if topo.may_write(e, d)]
            if direct:
                gs.append((("q", "b"), [(d, "b", 0, "fb", W * slot, W, "fb%d" % slot, m)
                                        for d, m in zip(direct, _share(offm, len(direct)))]))
            if e == relay[x]:
                for r in here[x]:
                    on = [d for d in far if not topo.may_write(r, d)]
                    if r != e and on:
                        s = seq[x].index(r)
                        gs.append((("rl", None), [(d, "rl", 0, "fb", W * s, W, "fb%d" % s, m)
                                                  for d, m in zip(on, _share(offm, len(on)))]))
            to = [d for d in execs[x] if d != e]
            for h, (lo, hi) in enumerate(pieces[e]):
                tr = []
                for d, m in zip(to, _share(chipm, len(to))):
                    s = foreign[d].index(e)
                    tr.append((d, "a", W * lo, "fa", 4 * W * s + W * lo, W * (hi - lo), "fa%d%d" % (s, h), m))
                gs.append((("q", "a%d" % h if len(pieces[e]) > 1 else "a1"), tr))
        for k, (_, _, _, c) in enumerate(jobs[e]):
            if c != e:
                s = sources[c].index(e)
                m = _share(upper if topo.chip(c) == x else offm, 1)[0]
                gs.append((("q", "p%d" % k), [(c, "p", W * k, "fp", W * s, W, "fp%d" % s, m)]))
        sends[e] = gs
    total = {}
    for e in sends:
        for _, tr in sends[e]:
            for d, _, _, _, _, _, s, m in tr:
                total[d, s] = total.get((d, s), 0) + 2 * len(_engines(m))
    return {"jobs": jobs, "foreign": foreign, "pieces": pieces, "sources": sources, "sends": sends, "total": total}


def rank_program(g, core, T, topo):
    P = _plan(T, topo)
    if core not in P["jobs"]:
        return
    is_rank = T.rank_of(core) is not None
    jobs, total = P["jobs"][core], P["total"]
    pe, vec, sca = g.tensor, g.vector, g.scalar
    Relu, Copy = ActivationFunctionType.Relu, ActivationFunctionType.Copy
    seen = {}

    def need(queue, name, sem, val):
        if seen.get((name, sem), 0) < val:
            seen[name, sem] = val
            queue.wait_ge(T.sem[sem], val)

    qn = {}

    def quantise(key, q, s, src):
        qn[key] = len(qn) + 1
        vec.quantize_mx(q, s, src).then_inc(T.sem.vq, 1)

    if is_rank:
        g.sync.dma_start(T.tb[:], T.b[:]).then_inc(T.sem.lb, 16)
        for h in range(2):
            g.sync.dma_start(T.ta[:, 1024 * h:1024 * h + 1024], T.a[:, 1024 * h:1024 * h + 1024]).then_inc(T.sem["la%d" % h], 16)
        vec.memset(T.dsel[:], 1.0).then_inc(T.sem.ms, 1)
        g.wait_ge(T.sem.ms, 1)
        g.affine_select(T.dsel[:], T.dsel[:], [[-1, 516]], AluOpType.is_equal, 0.0, 3, 4).then_inc(T.sem.ds, 1)
        vec.wait_ge(T.sem.lb, 16)
        quantise("b", T.qb[:], T.sb[:], T.tb[:])
        for h in range(2):
            vec.wait_ge(T.sem["la%d" % h], 16)
            quantise("a%d" % h, T.qa[:, 256 * h:256 * h + 256], T.sa[:, 256 * h:256 * h + 256], T.ta[:, 1024 * h:1024 * h + 1024])
        vec.wait_ge(T.sem.ds, 1)
        for i in range(4):
            quantise("s%d" % i, T.qsel[:, W * i:W * i + W], T.ssel[:, W * i:W * i + W], T.dsel[:, 3 - i:515 - i])

    np_, ns, na = 0, 0, 0
    wide = 0
    for k, (kind, slot, who, owner) in enumerate(jobs):
        order = [(i, w) for i in range(4) for w in range(len(who))]
        if len(who) > 1:
            if not wide:
                order = [(i, w) for w in range(len(who)) for i in range(4)]
            wide += 1
        mv = {"rl": (T.qrl, T.srl), "fb": (T.qfb, T.sfb), "b": (T.qb, T.sb)}[kind]
        done = {}
        for i, w in order:
            r = who[w]
            if r == core:
                need(pe, "pe", "vq", qn["a%d" % (i // 2)])
                lq, ls = T.qa[:, W * i:W * i + W], T.sa[:, W * i:W * i + W]
            else:
                s = P["foreign"][core].index(r)
                h = [n for n, (lo, hi) in enumerate(P["pieces"][r]) if lo <= i < hi][0]
                name = "fa%d%d" % (s, h)
                need(pe, "pe", name, total[core, name])
                o = 4 * W * s + W * i
                lq, ls = T.qfa[:, o:o + W], T.sfa[:, o:o + W]
            if kind == "b":
                need(pe, "pe", "vq", qn["b"])
            else:
                name = "rl" if kind == "rl" else "fb%d" % slot
                need(pe, "pe", name, total[core, name])
            if np_ >= RING:
                need(pe, "pe", "sc", np_ - RING + 1)
            bank = T.pr[:, 512 * (np_ % RING):512 * (np_ % RING) + W]
            pe.matmul_mx(bank, lq, ls, mv[0][:, W * slot:W * slot + W], mv[1][:, W * slot:W * slot + W], True, True).then_inc(T.sem.pe, 1)
            np_ += 1
            need(sca, "sca", "pe", np_)
            if len(who) == 1:
                out = T.tile[:, 512 * k + i:512 * k + 512:4]
            else:
                o = 512 * (2 * k + w) + W * i
                out = T.t[:, o:o + W]
            sca.activation(out, bank, Relu).then_inc(T.sem.sc, 1)
            ns += 1
            done[i, w] = ns
            if len(who) > 1 and len([1 for v in range(len(who)) if (i, v) in done]) == len(who):
                need(vec, "vec", "sc", ns)
                o0, o1 = 1024 * k + W * i, 1024 * k + 512 + W * i
                vec.tensor_tensor(T.tile[:, 512 * k + i:512 * k + 512:4], T.t[:, o0:o0 + W], T.t[:, o1:o1 + W], AluOpType.add).then_inc(T.sem.va, 1)
                na += 1
        if len(who) > 1:
            need(vec, "vec", "va", na)
        else:
            need(vec, "vec", "sc", ns)
        quantise("p%d" % k, T.qp[:, W * k:W * k + W], T.sp[:, W * k:W * k + W], T.tile[:, 512 * k:512 * k + 512])

    nsent = 0
    for (what, key), tr in P["sends"][core]:
        if what == "q":
            need(g, "g", "vq", qn[key])
        else:
            need(g, "g", what, total[core, what])
        for codes in (True, False):
            ts = []
            for d, fk, f0, tk, t0, w, sem, m in tr:
                nsent += len(_engines(m))
                if codes:
                    src = T["q" + fk][:, f0:f0 + w].bitcast(dt.uint8)
                    dst = T["q" + tk][:, t0:t0 + w].bitcast(dt.uint8)
                else:
                    src, dst = T["s" + fk][:, f0:f0 + w], T["s" + tk][:, t0:t0 + w]
                ts.append((d, src, dst, sem, m))
            if len(ts) == 1:
                d, src, dst, sem, m = ts[0]
                rid, pid, _ = topo.addr(d)
                g.remote_dma(out_ap=dst, in_ap=src, remote_sem=T.sem[sem], local_sem=T.sem.sent, pid=pid, routing_id=rid, dma_engine_mask=m)
            else:
                g.remote_dma_fused([RemoteDMATransfer(dst_ids=[DstId(rid=topo.addr(d)[0], pnc=topo.addr(d)[1])], dma_engine_mask=m,
                                                      remote_sem=T.sem[sem], src=src, dst=dst) for d, src, dst, sem, m in ts],
                                   local_sem=T.sem.sent)
    g.wait_ge(T.sem.sent, nsent)

    if is_rank:
        tiles = [("p", len(jobs) - 1, None)] + [("fp", s, "fp%d" % s) for s in range(len(P["sources"][core]))]
        for n, (kind, s, sem) in enumerate(tiles):
            if sem is None:
                need(pe, "pe", "vq", qn["p%d" % s])
            else:
                need(pe, "pe", sem, total[core, sem])
            last = n == len(tiles) - 1
            for i in range(4):
                mm = pe.matmul_mx(T.fin[:, 512 * i:512 * i + W], T.qsel[:, W * i:W * i + W], T.ssel[:, W * i:W * i + W],
                                  T["q" + kind][:, W * s:W * s + W], T["s" + kind][:, W * s:W * s + W], n == 0, last)
                if last:
                    mm.then_inc(T.sem.fin, 1)
        for i in range(4):
            bank, out = T.fin[:, 512 * i:512 * i + W], T.yt[:, i:512:4]
            if i % 2 == 0:
                sca.wait_ge(T.sem.fin, i + 1)
                sca.activation(out, bank, Copy).then_inc(T.sem.yd, 1)
            else:
                vec.wait_ge(T.sem.fin, i + 1)
                vec.tensor_copy(out, bank).then_inc(T.sem.yd, 1)
        g.sync.wait_ge(T.sem.yd, 4)
        g.sync.dma_start(T.y[:], T.yt[:]).then_inc(T.sem.st, 16)
        g.sync.wait_ge(T.sem.st, 16)
